import numpy as np, ml_dtypes
CORES = [7,15,23,39,47,63,71,79,87,95,119,127]
N = 12
R, C = 2, 512
def setup_inputs(rng):
    return {"x": rng.standard_normal((N, 128, C), dtype=np.float32).astype(ml_dtypes.bfloat16), "u": rng.standard_normal((N, R, 128), dtype=np.float32).astype(ml_dtypes.bfloat16), "v": rng.standard_normal((N, R, C), dtype=np.float32).astype(ml_dtypes.bfloat16)}
def setup_inputs_big(rng):
    d = setup_inputs(rng)
    for k in ("u", "v"): d[k] = (d[k].astype(np.float32) * 1024.0).astype(d[k].dtype)
    for k in ("x",): d[k] = (d[k].astype(np.float32) * 1024.0 ** 2).astype(d[k].dtype)
    return d
def setup_inputs_small(rng):
    d = setup_inputs(rng)
    for k in ("u", "v"): d[k] = (d[k].astype(np.float32) * (1 / 1024.0)).astype(d[k].dtype)
    for k in ("x",): d[k] = (d[k].astype(np.float32) * (1 / 1024.0 ** 2)).astype(d[k].dtype)
    return d
def setup_inputs_apart(rng):
    d = setup_inputs(rng)
    f = (10.0 ** rng.permutation(np.linspace(-1.5, 1.5, N))).astype(np.float32).reshape(N, 1, 1)
    for k in ("u", "v"): d[k] = (d[k].astype(np.float32) * f).astype(d[k].dtype)
    for k in ("x",): d[k] = (d[k].astype(np.float32) * f * f).astype(d[k].dtype)
    return d
def reference(x, u, v):
    X, U, V = x.astype(np.float64), u.astype(np.float64), v.astype(np.float64)
    s = V.sum(axis=0)
    return {"y": np.stack([X[r] + U[r].T @ s for r in range(N)]).astype(ml_dtypes.bfloat16 if x.dtype != np.float64 else np.float64)}

from concourse.bass import DstId, RemoteDMATransfer
from concourse.mybir import AluOpType

N, R, C, M = 12, 2, 512, 128
K = N * R
NENG = 4
NCH = 4
CW = C // NCH

SCRATCH = {
    "gath": ("dram", [N, 128, R * C // 128], "bfloat16"),
    "G": ("sbuf", [128, C], "bfloat16"),
    "usb": ("sbuf", [128, R * M], "bfloat16"),
    "E": ("sbuf", [128, 64], "bfloat16"),
    "U": ("sbuf", [128, M], "bfloat16"),
    "xsb": ("sbuf", [128, C], "bfloat16"),
    "ysb": ("sbuf", [128, C], "bfloat16"),
    "psu": ("psum", [128, 512], "float32"),
}
for _i in range(NCH):
    SCRATCH["ps%d" % _i] = ("psum", [128, 512], "float32")

SEMAPHORES = ["vcopied", "sent", "arrived", "gathered", "uloaded", "xloaded", "filled", "urep", "ustacked",
              "added", "stored"] + ["mm%d" % _i for _i in range(NCH)]


def _hops(topo, a, b):
    ca, cb = topo.chip(a), topo.chip(b)
    return 1 if (topo.mates(ca, cb) or topo.same_plane(ca, cb)) else 2


def rank_program(g, core, T, topo):
    rank = T.rank_of(core)
    if rank is None:
        return
    S = T.sem
    cores = T.cores

    g.sync.dma_start(T.gath[0], T.v[:]).then_inc(S.vcopied, 16)

    g.scalar.dma_start(T.usb[0:1, 0:R * M], T.u[:]).then_inc(S.uloaded, 16)
    g.scalar.dma_start(T.xsb[:], T.x[:]).then_inc(S.xloaded, 16)

    others = sorted((b for b in range(N) if b != rank),
                    key=lambda b: (-_hops(topo, core, cores[b]), (b - rank) % N))
    usable = -1
    for b in others:
        if not topo.may_write(core, cores[b]):
            raise ValueError("rank %d cannot write to rank %d directly" % (rank, b))
        usable &= topo.mask(core, cores[b])
    engines = [e for e in range(usable.bit_length()) if (usable >> e) & 1]
    engines = engines[::len(engines) // NENG][:NENG]
    transfers = []
    for k, e in enumerate(engines):
        mine = others[k::NENG]
        ids = []
        for b in mine:
            rid, pid, _se = topo.addr(cores[b])
            ids.append(DstId(rid=rid, pnc=pid))
        transfers.append(RemoteDMATransfer(dst_ids=ids, dma_engine_mask=1 << e, remote_sem=S.arrived,
                                           srcs=[T.gath[0]], dsts=[T.gath[(rank - b) % N] for b in mine], alu_op=0))
    g.wait_ge(S.vcopied, 16)
    g.remote_dma_fused(transfers, local_sem=S.sent)
    g.wait_ge(S.sent, NENG)

    g.sync.wait_ge(S.vcopied, 16)
    g.sync.wait_ge(S.arrived, N - 1)
    g.sync.dma_start(T.G[0:K, :], T.gath[:]).then_inc(S.gathered, 16)

    g.vector.memset(T.E[0:1, 0:K:2], 1.0).then_inc(S.filled, 1)
    g.vector.memset(T.E[0:1, 1:K:2], 0.0).then_inc(S.filled, 1)
    g.vector.memset(T.E[0:1, 32:32 + K:2], 0.0).then_inc(S.filled, 1)
    g.vector.memset(T.E[0:1, 33:32 + K:2], 1.0).then_inc(S.filled, 1)
    g.tensor.wait_ge(S.filled, 4)
    g.tensor.wait_ge(S.uloaded, 16)
    g.tensor.matmul(T.psu[0:K, 0:M], T.E[0:1, 0:K], T.usb[0:1, 0:M], True, False)
    g.tensor.matmul(T.psu[0:K, 0:M], T.E[0:1, 32:32 + K], T.usb[0:1, M:2 * M], False, True).then_inc(S.urep, 1)
    g.vector.wait_ge(S.urep, 1)
    g.vector.tensor_copy(T.U[0:K, :], T.psu[0:K, 0:M]).then_inc(S.ustacked, 1)

    g.tensor.wait_ge(S.ustacked, 1)
    g.tensor.wait_ge(S.gathered, 16)
    g.vector.wait_ge(S.xloaded, 16)
    for i in range(NCH):
        cols = slice(i * CW, (i + 1) * CW)
        ps = T["ps%d" % i]
        g.tensor.matmul(ps[:, 0:CW], T.U[0:K, :], T.G[0:K, cols], True, True).then_inc(S["mm%d" % i], 1)
        g.vector.wait_ge(S["mm%d" % i], 1)
        g.vector.tensor_tensor(T.ysb[:, cols], ps[:, 0:CW], T.xsb[:, cols], AluOpType.add).then_inc(S.added, 1)

    g.scalar.wait_ge(S.added, NCH)
    g.scalar.dma_start(T.y[:], T.ysb[:]).then_inc(S.stored, 16)
    g.scalar.wait_ge(S.stored, 16)
